import numpy as np
import ml_dtypes


def mxq(x, axis, fmt="e4m3"):
    dtype, down = {"e4m3": (ml_dtypes.float8_e4m3fn, 7), "e5m2": (ml_dtypes.float8_e5m2, 14)}[fmt]
    v = np.moveaxis(np.asarray(x, np.float32).astype(ml_dtypes.bfloat16).astype(np.float64), axis, -1)
    blocks = v.reshape(v.shape[:-1] + (-1, 32))
    amax = np.abs(blocks).max(-1, keepdims=True)
    byte = np.maximum(np.where(amax > 0, np.frexp(amax)[1] - 1 + 127, 0) - down, 1)
    scale = np.exp2(byte - 127.0)
    codes = (blocks / scale).astype(np.float32).astype(dtype).astype(np.float64)
    return np.moveaxis((codes * scale).reshape(v.shape), -1, axis)


WIDE = False


def mx_kscale(k):
    if not WIDE:
        return np.ones(k)
    levels = np.array([10, -10, 5, -5, 0])
    if k % 512:
        return np.exp2(np.random.permutation(np.resize(levels, k // 32))).repeat(32)
    a = np.empty((k // 512, 16))
    for p in range(k // 512):
        a[p, :8] = np.random.permutation(np.resize(levels, 8))
        for g in range(8):
            far = levels[np.abs(levels - a[p, g]) >= 10]
            a[p, g + 8] = far[np.random.randint(len(far))]
    return np.exp2(a.ravel()).repeat(32)


def f64(x):
    return np.asarray(x).astype(np.float64)


def striped(idx):
    return np.tile(idx.reshape(-1, 16).T, (8, 1)).astype(np.uint16)


def unstriped(offs):
    return offs[:16].T.reshape(-1).astype(np.int64)


def striped8(idx):
    return np.concatenate([x.reshape(-1, 16).T for x in idx]).astype(np.uint16)


def runs(offs, k):
    lists = np.stack([offs[16 * r : 16 * r + 16].T.reshape(-1) for r in range(8)]).astype(np.int64)
    return lists[np.arange(k) % 512 // 64]


def pack_weight(w):
    k, n = w.shape
    w = f64(np.asarray(w, np.float32).astype(ml_dtypes.bfloat16)).reshape(k // 32, 32, n)
    amax = np.abs(w).max(1)
    byte = np.clip(np.where(amax > 0, np.frexp(amax)[1] - 1 + 127 - 7, 1), 1, 254)
    scaled = (w * np.exp2(127.0 - byte)[:, None, :]).reshape(k, n).astype(np.float32)
    words = np.ascontiguousarray(scaled.reshape(k // 512, 128, 4, n).transpose(0, 1, 3, 2)).astype(ml_dtypes.float8_e4m3fn).view(np.uint8)
    return words, np.ascontiguousarray(byte.astype(np.uint8).reshape(k // 512, 16, n))


def unpack_weight(words, scales):
    g, p, n, _ = words.shape
    vals = np.ascontiguousarray(words).view(ml_dtypes.float8_e4m3fn).astype(np.float64) * np.repeat(np.exp2(scales.astype(np.float64) - 127.0), 8, axis=1)[..., None]
    return vals.transpose(0, 1, 3, 2).reshape(g * 512, n)


K, T, S, H, W, C = 512, 2048, 512, 512, 2048, 512


def setup_inputs():
    n = np.random.standard_normal
    s = mx_kscale(K)[:, None]
    packed_xT = pack_weight(n((K, T)) * s)
    return {
        "x_words": packed_xT[0],
        "x_scales": packed_xT[1],
        "w1": (n((K, H)) / np.sqrt(K) / s).astype(np.float32),
        "gs": (np.random.uniform(0.5, 1.5, (K, 1)) / s).astype(np.float32),
        "gs2": (np.random.uniform(0.5, 1.5, (K, 1)) / s).astype(np.float32),
        "offs": striped(np.random.permutation(T)[:S]),
        "n1": striped8(np.stack([np.random.permutation(S) for _ in range(8)])),
        "n2": striped8(np.stack([np.random.permutation(S) for _ in range(8)])),
        "n3": striped(np.random.randint(0, S, W)),
        "ca": striped(np.random.permutation(T)[:C]),
        "cb": striped(np.random.permutation(T)[:C]),
        "n4": striped(np.random.permutation(S)),
        "n5": striped(np.random.permutation(S)),
    }


def reference(x_words, x_scales, w1, gs, gs2, offs, n1, n2, n3, ca, cb, n4, n5):
    x_ca = unpack_weight(x_words, x_scales)[:, unstriped(ca)]
    xq = unpack_weight(x_words, x_scales)[:, unstriped(offs)]
    y = mxq(f64(w1), 0, "e4m3").T @ xq
    pa = y[np.arange(H)[:, None], runs(n1, H)]
    pb = y[np.arange(H)[:, None], runs(n2, H)]
    z = f64(gs) * (np.maximum(np.minimum(y, pa), np.minimum(np.maximum(y, pa), pb)))
    a = 0.0625 * ((x_ca.T @ mxq(z, 0, "e4m3")))
    x_cb = unpack_weight(x_words, x_scales)[:, unstriped(cb)]
    mb = y[:, unstriped(n3)]
    mx = mb.reshape(H, S, 4).max(axis=2)
    mn = mb.reshape(H, S, 4).min(axis=2)
    z2 = f64(gs2) * (mx * np.tanh(y - mn))
    b = 0.0625 * ((x_cb.T @ mxq(z2, 0, "e4m3")))
    return np.maximum(a, b[:, unstriped(n5)]) - (np.minimum(a[:, unstriped(n4)], b))

@@ -1,0 +1,226 @@
+from contextlib import ExitStack
+
+import concourse.mybir as mybir
+
+K, T, S, H, C = 512, 2048, 512, 512, 512
+FLOPS = 3 * 2 * 512 * 512 * 512
+
+F32 = mybir.dt.float32
+BF16 = mybir.dt.bfloat16
+I32 = mybir.dt.int32
+U32 = mybir.dt.uint32
+U16 = mybir.dt.uint16
+U8 = mybir.dt.uint8
+FP8X4 = mybir.dt.float8_e4m3fn_x4
+ALU = mybir.AluOpType
+ACT = mybir.ActivationFunctionType
+
+P = 128
+PACK = 4
+HALF = S // 2
+MEMBERS = 4
+SPARE = 16
+LINE = 4
+
+
+def tile_picked_twocdmaxbmedgtan_none_p_kernel(
+    tc, x_words, x_scales, w1, gs, gs2, offs, n1, n2, n3, ca, cb, n4, n5, out
+):
+    nc = tc.nc
+    with ExitStack() as ctx:
+        keep = ctx.enter_context(tc.tile_pool(name="keep", bufs=1))
+        ring = ctx.enter_context(tc.tile_pool(name="ring", bufs=2))
+        psum = ctx.enter_context(tc.psum_pool(name="psum", bufs=1))
+
+        def load_list(name, src):
+            tile = keep.tile(list(src.shape), U16, name=name)
+            nc.sync.dma_start(tile[:], src)
+            return tile
+
+        def entries(tile, first, count):
+            return tile[:, first // 16 : (first + count) // 16]
+
+        xs = keep.tile([P, T], U8, name="xs", align_bytes=64)
+        nc.gpsimd.memset(xs[:].bitcast(I32), 0)
+        offs_t = load_list("offs_t", offs)
+        for q in range(4):
+            nc.sync.dma_start(xs[32 * q : 32 * q + 4, :].bitcast(I32), x_scales[0, 4 * q : 4 * q + 4, :].bitcast(I32))
+        ca_t = load_list("ca_t", ca)
+        cb_t = load_list("cb_t", cb)
+        w_raw = keep.tile([P, PACK, H], F32, name="w_raw")
+        nc.sync.dma_start(w_raw[:], w1.rearrange("(p j) c -> p j c", j=PACK))
+        xw = keep.tile([P, T], I32, name="xw", align_bytes=64)
+        nc.sync.dma_start(xw[:], x_words[0].rearrange("p n t -> p (n t)").bitcast(I32))
+        g2 = keep.tile([P, PACK], F32, name="g2")
+        nc.sync.dma_start(g2[:], gs2.rearrange("(p t) o -> p (t o)", t=PACK))
+        g1 = keep.tile([P, PACK], F32, name="g1")
+        nc.sync.dma_start(g1[:], gs.rearrange("(p t) o -> p (t o)", t=PACK))
+        n3_t = load_list("n3_t", n3)
+        n2_t = load_list("n2_t", n2)
+        n1_t = load_list("n1_t", n1)
+        n4_t = load_list("n4_t", n4)
+        n5_t = load_list("n5_t", n5)
+
+        def pick_bytes(name, lst):
+            tile = keep.tile([P, S], U8, name=name, align_bytes=64)
+            nc.vector.tensor_copy(tile[:], xs[:].indirect(lst[:]))
+            return tile
+
+        def pick_words(name, lst):
+            tile = keep.tile([P, S], U32, name=name, align_bytes=64)
+            nc.vector.tensor_copy(tile[:], xw[:].bitcast(U32).indirect(lst[:]))
+            return tile
+
+        xq_s = pick_bytes("xq_s", offs_t)
+        ca_s = pick_bytes("ca_s", ca_t)
+        cb_s = pick_bytes("cb_s", cb_t)
+
+        w_bf = keep.tile([P, PACK, P, PACK], BF16, name="w_bf", align_bytes=64)
+        nc.scalar.copy(w_bf[:].rearrange("p t m j -> p m j t"), w_raw[:].rearrange("p j (m t) -> p m j t", t=PACK))
+        w_c = keep.tile([P, H], U32, name="w_c", align_bytes=64)
+        w_s = keep.tile([P, H], U8, name="w_s", align_bytes=64)
+        nc.vector.quantize_mx(out=w_c[:].bitcast(FP8X4), scales=w_s[:], in_=w_bf[:].rearrange("p t m j -> p (t m j)"))
+        xq_w = pick_words("xq_w", offs_t)
+
+        g2_neg = keep.tile([P, PACK], F32, name="g2_neg")
+        g2_abs = keep.tile([P, PACK], F32, name="g2_abs")
+        g2_floor = keep.tile([P, PACK], F32, name="g2_floor")
+        g2_rec = keep.tile([P, PACK], F32, name="g2_rec")
+        g2_sign = keep.tile([P, PACK], F32, name="g2_sign")
+        g2_inv = keep.tile([P, PACK], F32, name="g2_inv")
+        nc.vector.tensor_scalar(g2_neg[:], g2[:], -1.0, None, ALU.mult)
+        nc.vector.tensor_scalar(g2_sign[:], g2[:], 0.0, 2.0, ALU.is_ge, ALU.mult)
+        nc.vector.tensor_tensor(g2_abs[:], g2[:], g2_neg[:], ALU.max)
+        nc.vector.tensor_scalar(g2_floor[:], g2_abs[:], 2.0**-126, None, ALU.max)
+        nc.vector.reciprocal(g2_rec[:], g2_floor[:])
+        nc.vector.scalar_tensor_tensor(g2_inv[:], g2_sign[:], -1.0, g2_rec[:], ALU.add, ALU.mult)
+
+        def mx_product(bank, lhs_w, lhs_s, tile_no, rhs_w, rhs_s):
+            cols = slice(P * tile_no, P * (tile_no + 1))
+            nc.tensor.matmul_mx(
+                out=bank,
+                lhsT=lhs_w[:, cols].bitcast(FP8X4),
+                lhsT_scale=lhs_s[:, cols],
+                rhs=rhs_w.bitcast(FP8X4),
+                rhs_scale=rhs_s,
+                start=True,
+                stop=True,
+            )
+
+        y_ps = [psum.tile([P, S], F32, name=f"y_ps{t}", tag=f"yb{t}") for t in range(PACK)]
+        for t in range(PACK):
+            mx_product(y_ps[t][:], w_c, w_s, t, xq_w[:], xq_s[:])
+        ca_w = pick_words("ca_w", ca_t)
+
+        y1 = [keep.tile([P, S], F32, name=f"y1_{t}") for t in range(PACK)]
+        y2 = [keep.tile([P, S + SPARE], F32, name=f"y2_{t}") for t in range(PACK)]
+        for t in range(PACK):
+            nc.gpsimd.memset(y2[t][:, S:], 0.0)
+        y1_bf = keep.tile([P, PACK, S], BF16, name="y1_bf")
+        pa = keep.tile([P, PACK, S], BF16, name="pa")
+        pb = keep.tile([P, PACK, S], BF16, name="pb")
+        lo = keep.tile([P, PACK, S], BF16, name="lo")
+        hi = keep.tile([P, PACK, S], BF16, name="hi")
+        mid = keep.tile([P, PACK, S], BF16, name="mid")
+        mx = [keep.tile([P, PACK, HALF], F32, name=f"mx{h}") for h in range(2)]
+        th = [keep.tile([P, PACK, HALF], F32, name=f"th{h}") for h in range(2)]
+
+        def fetch_members(t, h):
+            mb = ring.tile([P, HALF, MEMBERS], F32, name="mb")
+            flat = mb[:].rearrange("p j m -> p (j m)")
+            for first in range(0, HALF * MEMBERS, S):
+                lst = entries(n3_t, h * HALF * MEMBERS + first, S)
+                nc.scalar.activation(flat[:, first : first + S], y2[t][:].indirect(lst), ACT.Copy)
+            return mb
+
+        def reduce_members(t, h, mb):
+            big = ring.tile([P, HALF, 2], F32, name="big")
+            small = ring.tile([P, HALF, 2], F32, name="small")
+            mn = ring.tile([P, HALF], F32, name="mn")
+            diff = ring.tile([P, HALF], F32, name="diff")
+            nc.vector.tensor_tensor(small[:], mb[:, :, 0:2], mb[:, :, 2:4], ALU.min)
+            nc.vector.tensor_tensor(big[:], mb[:, :, 0:2], mb[:, :, 2:4], ALU.max)
+            nc.vector.tensor_tensor(mn[:], small[:, :, 0], small[:, :, 1], ALU.min)
+            nc.vector.tensor_tensor(mx[h][:, t, :], big[:, :, 0], big[:, :, 1], ALU.max)
+            nc.vector.tensor_tensor(diff[:], y2[t][:, h * HALF : (h + 1) * HALF], mn[:], ALU.subtract)
+            return diff
+
+        def squash(t, h, diff):
+            nc.scalar.activation(th[h][:, t, :], diff[:], ACT.Tanh, scale=g2_inv[:, t : t + 1])
+
+        def weave_and_quantize(name, in0, in1, op, width):
+            woven = keep.tile([P, width, PACK], BF16, name=f"{name}_bf", align_bytes=64)
+            nc.vector.tensor_tensor(
+                woven[:].rearrange("p (c i) t -> p c t i", i=LINE),
+                in0.rearrange("p t (c i) -> p c t i", i=LINE),
+                in1.rearrange("p t (c i) -> p c t i", i=LINE),
+                op,
+            )
+            codes = keep.tile([P, width], U32, name=f"{name}_c", align_bytes=64)
+            scales = keep.tile([P, width], U8, name=f"{name}_s", align_bytes=64)
+            nc.vector.quantize_mx(out=codes[:].bitcast(FP8X4), scales=scales[:], in_=woven[:].rearrange("p j t -> p (j t)"))
+            return codes, scales
+
+        diffs = {}
+        for t in range(PACK):
+            nc.scalar.activation(y2[t][:, :S], y_ps[t][:], ACT.Copy, scale=g2_abs[:, t : t + 1])
+            nc.vector.tensor_scalar(y1[t][:], y_ps[t][:], g1[:, t : t + 1], None, ALU.mult)
+            mb = fetch_members(t, 0)
+            for first in (0, HALF):
+                nc.scalar.activation(pa[:, t, first : first + HALF], y1[t][:].indirect(entries(n1_t, first, HALF)), ACT.Copy)
+            for first in (0, HALF):
+                nc.vector.tensor_copy(pb[:, t, first : first + HALF], y1[t][:].indirect(entries(n2_t, first, HALF)))
+            nc.vector.tensor_copy(y1_bf[:, t, :], y1[t][:])
+            if t > 0:
+                squash(t - 1, 0, diffs[t - 1, 0])
+            diffs[t, 0] = reduce_members(t, 0, mb)
+            nc.vector.tensor_tensor(hi[:, t, :], y1_bf[:, t, :], pa[:, t, :], ALU.max)
+            nc.vector.tensor_tensor(lo[:, t, :], y1_bf[:, t, :], pa[:, t, :], ALU.min)
+            nc.vector.tensor_tensor(mid[:, t, :], hi[:, t, :], pb[:, t, :], ALU.min)
+
+        a_ps = [psum.tile([P, S], F32, name=f"a_ps{c}", tag=f"a{c}") for c in range(PACK)]
+        b_ps = [psum.tile([P, S], F32, name=f"b_ps{c}", tag=f"yb{c}") for c in range(PACK)]
+
+        def score_b(h, cb_w):
+            z2_c, z2_s = weave_and_quantize(f"z2_{h}", mx[h][:], th[h][:], ALU.mult, HALF)
+            for c in range(PACK):
+                mx_product(b_ps[c][:, h * HALF : (h + 1) * HALF], cb_w, cb_s, c, z2_c[:], z2_s[:])
+
+        for t in range(PACK):
+            mb = fetch_members(t, 1)
+            squash(*((PACK - 1, 0) if t == 0 else (t - 1, 1)), diffs[(PACK - 1, 0) if t == 0 else (t - 1, 1)])
+            if t == 0:
+                z_c, z_s = weave_and_quantize("z", lo[:], mid[:], ALU.max, S)
+                for c in range(PACK):
+                    mx_product(a_ps[c][:], ca_w, ca_s, c, z_c[:], z_s[:])
+            if t == 1:
+                cb_w = pick_words("cb_w", cb_t)
+            if t == 2:
+                score_b(0, cb_w)
+            diffs[t, 1] = reduce_members(t, 1, mb)
+
+        a_sb = [keep.tile([P, S], F32, name=f"a_sb{c}") for c in range(PACK)]
+        b_sb = [keep.tile([P, S], F32, name=f"b_sb{c}") for c in range(PACK)]
+        a4 = keep.tile([P, PACK, S], F32, name="a4")
+        b5 = keep.tile([P, PACK, S], F32, name="b5")
+
+        def leave_and_fetch(bank, window, lst, fetched):
+            nc.scalar.activation(window[:], bank[:], ACT.Copy, scale=0.0625)
+            for first in (0, HALF):
+                nc.scalar.activation(fetched[:, first : first + HALF], window[:].indirect(entries(lst, first, HALF)), ACT.Copy)
+
+        leave_and_fetch(a_ps[0], a_sb[0], n4_t, a4[:, 0, :])
+        squash(PACK - 1, 1, diffs[PACK - 1, 1])
+        score_b(1, cb_w)
+        for c in range(1, PACK):
+            leave_and_fetch(a_ps[c], a_sb[c], n4_t, a4[:, c, :])
+
+        for c in range(PACK):
+            leave_and_fetch(b_ps[c], b_sb[c], n5_t, b5[:, c, :])
+            less = ring.tile([P, S], F32, name="less")
+            more = ring.tile([P, S], F32, name="more")
+            res = ring.tile([P, S], F32, name="res")
+            nc.vector.tensor_tensor(less[:], a4[:, c, :], b_sb[c][:], ALU.min)
+            nc.vector.tensor_tensor(more[:], a_sb[c][:], b5[:, c, :], ALU.max)
+            nc.vector.tensor_tensor(res[:], more[:], less[:], ALU.subtract)
+            nc.sync.dma_start(out[P * c : P * (c + 1), :], res[:])

@@ -21,6 +21,7 @@ HALF = S // 2
 MEMBERS = 4
 SPARE = 16
 LINE = 4
+LATE = 2
 
 
 def tile_picked_twocdmaxbmedgtan_none_p_kernel(
@@ -43,45 +44,37 @@ def tile_picked_twocdmaxbmedgtan_none_p_kernel(
         xs = keep.tile([P, T], U8, name="xs", align_bytes=64)
         nc.gpsimd.memset(xs[:].bitcast(I32), 0)
         offs_t = load_list("offs_t", offs)
-        for q in range(4):
-            nc.sync.dma_start(xs[32 * q : 32 * q + 4, :].bitcast(I32), x_scales[0, 4 * q : 4 * q + 4, :].bitcast(I32))
         ca_t = load_list("ca_t", ca)
-        cb_t = load_list("cb_t", cb)
-        w_raw = keep.tile([P, PACK, H], F32, name="w_raw")
-        nc.sync.dma_start(w_raw[:], w1.rearrange("(p j) c -> p j c", j=PACK))
-        xw = keep.tile([P, T], I32, name="xw", align_bytes=64)
-        nc.sync.dma_start(xw[:], x_words[0].rearrange("p n t -> p (n t)").bitcast(I32))
         g2 = keep.tile([P, PACK], F32, name="g2")
         nc.sync.dma_start(g2[:], gs2.rearrange("(p t) o -> p (t o)", t=PACK))
+        for q in range(4):
+            nc.sync.dma_start(xs[32 * q : 32 * q + 4, :].bitcast(I32), x_scales[0, 4 * q : 4 * q + 4, :].bitcast(I32))
+        xw = keep.tile([P, T], I32, name="xw", align_bytes=64)
+        nc.sync.dma_start(xw[:], x_words[0].rearrange("p n t -> p (n t)").bitcast(I32))
+        w_raw = [keep.tile([P, PACK, H // 2], F32, name=f"w_raw{u}") for u in range(2)]
+        for u in range(2):
+            nc.sync.dma_start(w_raw[u][:], w1.rearrange("(p j) c -> p j c", j=PACK)[:, :, u * (H // 2) : (u + 1) * (H // 2)])
+        n3_t = load_list("n3_t", n3)
         g1 = keep.tile([P, PACK], F32, name="g1")
         nc.sync.dma_start(g1[:], gs.rearrange("(p t) o -> p (t o)", t=PACK))
-        n3_t = load_list("n3_t", n3)
         n2_t = load_list("n2_t", n2)
         n1_t = load_list("n1_t", n1)
+        cb_t = load_list("cb_t", cb)
         n4_t = load_list("n4_t", n4)
         n5_t = load_list("n5_t", n5)
 
-        def pick_bytes(name, lst):
-            tile = keep.tile([P, S], U8, name=name, align_bytes=64)
+        def pick_bytes(name, lst, tag):
+            tile = keep.tile([P, S], U8, name=name, tag=tag, align_bytes=64)
             nc.vector.tensor_copy(tile[:], xs[:].indirect(lst[:]))
             return tile
 
-        def pick_words(name, lst):
-            tile = keep.tile([P, S], U32, name=name, align_bytes=64)
+        def pick_words(name, lst, tag):
+            tile = keep.tile([P, S], U32, name=name, tag=tag, align_bytes=64)
             nc.vector.tensor_copy(tile[:], xw[:].bitcast(U32).indirect(lst[:]))
             return tile
 
-        xq_s = pick_bytes("xq_s", offs_t)
-        ca_s = pick_bytes("ca_s", ca_t)
-        cb_s = pick_bytes("cb_s", cb_t)
-
-        w_bf = keep.tile([P, PACK, P, PACK], BF16, name="w_bf", align_bytes=64)
-        nc.scalar.copy(w_bf[:].rearrange("p t m j -> p m j t"), w_raw[:].rearrange("p j (m t) -> p m j t", t=PACK))
-        w_c = keep.tile([P, H], U32, name="w_c", align_bytes=64)
-        w_s = keep.tile([P, H], U8, name="w_s", align_bytes=64)
-        nc.vector.quantize_mx(out=w_c[:].bitcast(FP8X4), scales=w_s[:], in_=w_bf[:].rearrange("p t m j -> p (t m j)"))
-        xq_w = pick_words("xq_w", offs_t)
-
+        xq_s = pick_bytes("xq_s", offs_t, "xq_s")
+        ca_s = pick_bytes("ca_s", ca_t, "ca_s")
         g2_neg = keep.tile([P, PACK], F32, name="g2_neg")
         g2_abs = keep.tile([P, PACK], F32, name="g2_abs")
         g2_floor = keep.tile([P, PACK], F32, name="g2_floor")
@@ -94,6 +87,25 @@ def tile_picked_twocdmaxbmedgtan_none_p_kernel(
         nc.vector.tensor_scalar(g2_floor[:], g2_abs[:], 2.0**-126, None, ALU.max)
         nc.vector.reciprocal(g2_rec[:], g2_floor[:])
         nc.vector.scalar_tensor_tensor(g2_inv[:], g2_sign[:], -1.0, g2_rec[:], ALU.add, ALU.mult)
+
+        xq_w = pick_words("xq_w", offs_t, "words")
+        ca_w = pick_words("ca_w", ca_t, "ca_w")
+
+        w_bf = keep.tile([P, PACK, P, PACK], BF16, name="w_bf", align_bytes=64)
+        def deal(copy, u, first, last):
+            copy(
+                w_bf[:, :, u * (P // 2) + first : u * (P // 2) + last, :].rearrange("p t m j -> p m j t"),
+                w_raw[u][:, :, PACK * first : PACK * last].rearrange("p j (m t) -> p m j t", t=PACK),
+            )
+
+        deal(nc.scalar.copy, 0, 0, P // 2)
+        deal(nc.scalar.copy, 1, 0, 24)
+        deal(nc.vector.tensor_copy, 1, 24, P // 2)
+        w_c = keep.tile([P, H], U32, name="w_c", align_bytes=64)
+        w_s = keep.tile([P, H], U8, name="w_s", align_bytes=64)
+        for t in range(PACK):
+            cols = slice(P * t, P * (t + 1))
+            nc.vector.quantize_mx(out=w_c[:, cols].bitcast(FP8X4), scales=w_s[:, cols], in_=w_bf[:, t].rearrange("p m j -> p (m j)"))
 
         def mx_product(bank, lhs_w, lhs_s, tile_no, rhs_w, rhs_s):
             cols = slice(P * tile_no, P * (tile_no + 1))
@@ -110,12 +122,15 @@ def tile_picked_twocdmaxbmedgtan_none_p_kernel(
         y_ps = [psum.tile([P, S], F32, name=f"y_ps{t}", tag=f"yb{t}") for t in range(PACK)]
         for t in range(PACK):
             mx_product(y_ps[t][:], w_c, w_s, t, xq_w[:], xq_s[:])
-        ca_w = pick_words("ca_w", ca_t)
 
-        y1 = [keep.tile([P, S], F32, name=f"y1_{t}") for t in range(PACK)]
-        y2 = [keep.tile([P, S + SPARE], F32, name=f"y2_{t}") for t in range(PACK)]
-        for t in range(PACK):
-            nc.gpsimd.memset(y2[t][:, S:], 0.0)
+        def window(name, width):
+            tile = keep.tile([P, width], F32, name=name)
+            nc.gpsimd.memset(tile[:, S:], 0.0)
+            return tile
+
+        y2 = [window(f"y2_{t}", HALF * MEMBERS + SPARE) for t in range(PACK)]
+        y1 = [window(f"y1_{t}", 2 * S) for t in range(PACK)]
+        a_sb, b_sb = y2, y1
         y1_bf = keep.tile([P, PACK, S], BF16, name="y1_bf")
         pa = keep.tile([P, PACK, S], BF16, name="pa")
         pb = keep.tile([P, PACK, S], BF16, name="pb")
@@ -126,18 +141,16 @@ def tile_picked_twocdmaxbmedgtan_none_p_kernel(
         th = [keep.tile([P, PACK, HALF], F32, name=f"th{h}") for h in range(2)]
 
         def fetch_members(t, h):
-            mb = ring.tile([P, HALF, MEMBERS], F32, name="mb")
-            flat = mb[:].rearrange("p j m -> p (j m)")
-            for first in range(0, HALF * MEMBERS, S):
-                lst = entries(n3_t, h * HALF * MEMBERS + first, S)
-                nc.scalar.activation(flat[:, first : first + S], y2[t][:].indirect(lst), ACT.Copy)
+            mb = ring.tile([P, HALF, MEMBERS], F32, name="mb", bufs=5)
+            lst = entries(n3_t, h * HALF * MEMBERS, HALF * MEMBERS)
+            nc.scalar.activation(mb[:].rearrange("p j m -> p (j m)"), y2[t][:].indirect(lst), ACT.Copy)
             return mb
 
         def reduce_members(t, h, mb):
             big = ring.tile([P, HALF, 2], F32, name="big")
             small = ring.tile([P, HALF, 2], F32, name="small")
             mn = ring.tile([P, HALF], F32, name="mn")
-            diff = ring.tile([P, HALF], F32, name="diff")
+            diff = ring.tile([P, HALF], F32, name="diff", bufs=4)
             nc.vector.tensor_tensor(small[:], mb[:, :, 0:2], mb[:, :, 2:4], ALU.min)
             nc.vector.tensor_tensor(big[:], mb[:, :, 0:2], mb[:, :, 2:4], ALU.max)
             nc.vector.tensor_tensor(mn[:], small[:, :, 0], small[:, :, 1], ALU.min)
@@ -161,66 +174,64 @@ def tile_picked_twocdmaxbmedgtan_none_p_kernel(
             nc.vector.quantize_mx(out=codes[:].bitcast(FP8X4), scales=scales[:], in_=woven[:].rearrange("p j t -> p (j t)"))
             return codes, scales
 
-        diffs = {}
         for t in range(PACK):
             nc.scalar.activation(y2[t][:, :S], y_ps[t][:], ACT.Copy, scale=g2_abs[:, t : t + 1])
-            nc.vector.tensor_scalar(y1[t][:], y_ps[t][:], g1[:, t : t + 1], None, ALU.mult)
-            mb = fetch_members(t, 0)
-            for first in (0, HALF):
-                nc.scalar.activation(pa[:, t, first : first + HALF], y1[t][:].indirect(entries(n1_t, first, HALF)), ACT.Copy)
-            for first in (0, HALF):
-                nc.vector.tensor_copy(pb[:, t, first : first + HALF], y1[t][:].indirect(entries(n2_t, first, HALF)))
-            nc.vector.tensor_copy(y1_bf[:, t, :], y1[t][:])
-            if t > 0:
-                squash(t - 1, 0, diffs[t - 1, 0])
-            diffs[t, 0] = reduce_members(t, 0, mb)
-            nc.vector.tensor_tensor(hi[:, t, :], y1_bf[:, t, :], pa[:, t, :], ALU.max)
-            nc.vector.tensor_tensor(lo[:, t, :], y1_bf[:, t, :], pa[:, t, :], ALU.min)
-            nc.vector.tensor_tensor(mid[:, t, :], hi[:, t, :], pb[:, t, :], ALU.min)
+            nc.vector.tensor_scalar(y1[t][:, :S], y_ps[t][:], g1[:, t : t + 1], None, ALU.mult)
+        for t in range(PACK):
+            (nc.scalar.copy if t < 1 else nc.vector.tensor_copy)(y1_bf[:, t, :], y1[t][:, :S])
+            nc.scalar.activation(pa[:, t, :], y1[t][:].indirect(n1_t[:]), ACT.Copy)
+            nc.vector.tensor_copy(pb[:, t, :], y1[t][:].indirect(n2_t[:]))
+        cb_s = pick_bytes("cb_s", cb_t, "w_bf")
+        cb_w = pick_words("cb_w", cb_t, "words")
+        for u in range(2):
+            rows = slice(2 * u, 2 * u + 2)
+            nc.vector.tensor_tensor(hi[:, rows, :], y1_bf[:, rows, :], pa[:, rows, :], ALU.max)
+            nc.vector.tensor_tensor(lo[:, rows, :], y1_bf[:, rows, :], pa[:, rows, :], ALU.min)
+            nc.vector.tensor_tensor(mid[:, rows, :], hi[:, rows, :], pb[:, rows, :], ALU.min)
 
         a_ps = [psum.tile([P, S], F32, name=f"a_ps{c}", tag=f"a{c}") for c in range(PACK)]
         b_ps = [psum.tile([P, S], F32, name=f"b_ps{c}", tag=f"yb{c}") for c in range(PACK)]
+        a4 = keep.tile([P, PACK, S], F32, name="a4")
+        b5 = keep.tile([P, PACK, S], F32, name="b5")
+        less = keep.tile([P, PACK, S], F32, name="less")
 
-        def score_b(h, cb_w):
+        def score_b(h):
             z2_c, z2_s = weave_and_quantize(f"z2_{h}", mx[h][:], th[h][:], ALU.mult, HALF)
             for c in range(PACK):
                 mx_product(b_ps[c][:, h * HALF : (h + 1) * HALF], cb_w, cb_s, c, z2_c[:], z2_s[:])
 
-        for t in range(PACK):
-            mb = fetch_members(t, 1)
-            squash(*((PACK - 1, 0) if t == 0 else (t - 1, 1)), diffs[(PACK - 1, 0) if t == 0 else (t - 1, 1)])
-            if t == 0:
-                z_c, z_s = weave_and_quantize("z", lo[:], mid[:], ALU.max, S)
-                for c in range(PACK):
-                    mx_product(a_ps[c][:], ca_w, ca_s, c, z_c[:], z_s[:])
-            if t == 1:
-                cb_w = pick_words("cb_w", cb_t)
-            if t == 2:
-                score_b(0, cb_w)
-            diffs[t, 1] = reduce_members(t, 1, mb)
+        def leave_and_fetch_a(c):
+            nc.scalar.activation(a_sb[c][:, :S], a_ps[c][:], ACT.Copy, scale=0.0625)
+            nc.scalar.activation(a4[:, c, :], a_sb[c][:].indirect(n4_t[:]), ACT.Copy)
 
-        a_sb = [keep.tile([P, S], F32, name=f"a_sb{c}") for c in range(PACK)]
-        b_sb = [keep.tile([P, S], F32, name=f"b_sb{c}") for c in range(PACK)]
-        a4 = keep.tile([P, PACK, S], F32, name="a4")
-        b5 = keep.tile([P, PACK, S], F32, name="b5")
-
-        def leave_and_fetch(bank, window, lst, fetched):
-            nc.scalar.activation(window[:], bank[:], ACT.Copy, scale=0.0625)
-            for first in (0, HALF):
-                nc.scalar.activation(fetched[:, first : first + HALF], window[:].indirect(entries(lst, first, HALF)), ACT.Copy)
-
-        leave_and_fetch(a_ps[0], a_sb[0], n4_t, a4[:, 0, :])
-        squash(PACK - 1, 1, diffs[PACK - 1, 1])
-        score_b(1, cb_w)
-        for c in range(1, PACK):
-            leave_and_fetch(a_ps[c], a_sb[c], n4_t, a4[:, c, :])
-
+        z_c, z_s = weave_and_quantize("z", lo[:], mid[:], ALU.max, S)
         for c in range(PACK):
-            leave_and_fetch(b_ps[c], b_sb[c], n5_t, b5[:, c, :])
-            less = ring.tile([P, S], F32, name="less")
-            more = ring.tile([P, S], F32, name="more")
-            res = ring.tile([P, S], F32, name="res")
-            nc.vector.tensor_tensor(less[:], a4[:, c, :], b_sb[c][:], ALU.min)
-            nc.vector.tensor_tensor(more[:], a_sb[c][:], b5[:, c, :], ALU.max)
-            nc.vector.tensor_tensor(res[:], more[:], less[:], ALU.subtract)
-            nc.sync.dma_start(out[P * c : P * (c + 1), :], res[:])
+            mx_product(a_ps[c][:], ca_w, ca_s, c, z_c[:], z_s[:])
+        for h in range(2):
+            for t in range(PACK):
+                squash(t, h, reduce_members(t, h, fetch_members(t, h)))
+                if (h, t) == (1, LATE):
+                    score_b(0)
+        score_b(1)
+        for c in range(PACK):
+            leave_and_fetch_a(c)
+
+        def leave_b(c):
+            nc.scalar.activation(b_sb[c][:, :S], b_ps[c][:], ACT.Copy, scale=0.0625)
+
+        leave_b(0)
+        for c in (1, 2, 0, 3):
+            nc.vector.scalar_tensor_tensor(less[:, c, :], b_ps[c][:], 0.0625, a4[:, c, :], ALU.mult, ALU.min)
+        for c in range(PACK):
+            if c > 0:
+                leave_b(c)
+            pieces = 2 if c == PACK - 1 else 1
+            width = S // pieces
+            for first in range(0, S, width):
+                cols = slice(first, first + width)
+                more = ring.tile([P, width], F32, name="more")
+                res = ring.tile([P, width], F32, name="res", bufs=5)
+                nc.scalar.activation(b5[:, c, cols], b_sb[c][:].indirect(entries(n5_t, first, width)), ACT.Copy)
+                nc.vector.tensor_tensor(more[:], a_sb[c][:, cols], b5[:, c, cols], ALU.max)
+                nc.vector.tensor_tensor(res[:], more[:], less[:, c, cols], ALU.subtract)
+                nc.sync.dma_start(out[P * c : P * (c + 1), cols], res[:])

@@ -22,6 +22,7 @@ MEMBERS = 4
 SPARE = 16
 LINE = 4
 LATE = 2
+DEAL_SPLIT = 40
 
 
 def tile_picked_twocdmaxbmedgtan_none_p_kernel(
@@ -51,9 +52,8 @@ def tile_picked_twocdmaxbmedgtan_none_p_kernel(
             nc.sync.dma_start(xs[32 * q : 32 * q + 4, :].bitcast(I32), x_scales[0, 4 * q : 4 * q + 4, :].bitcast(I32))
         xw = keep.tile([P, T], I32, name="xw", align_bytes=64)
         nc.sync.dma_start(xw[:], x_words[0].rearrange("p n t -> p (n t)").bitcast(I32))
-        w_raw = [keep.tile([P, PACK, H // 2], F32, name=f"w_raw{u}") for u in range(2)]
-        for u in range(2):
-            nc.sync.dma_start(w_raw[u][:], w1.rearrange("(p j) c -> p j c", j=PACK)[:, :, u * (H // 2) : (u + 1) * (H // 2)])
+        w_raw = keep.tile([P, PACK, H], F32, name="w_raw")
+        nc.sync.dma_start(w_raw[:], w1.rearrange("(p j) c -> p j c", j=PACK))
         n3_t = load_list("n3_t", n3)
         g1 = keep.tile([P, PACK], F32, name="g1")
         nc.sync.dma_start(g1[:], gs.rearrange("(p t) o -> p (t o)", t=PACK))
@@ -92,15 +92,11 @@ def tile_picked_twocdmaxbmedgtan_none_p_kernel(
         ca_w = pick_words("ca_w", ca_t, "ca_w")
 
         w_bf = keep.tile([P, PACK, P, PACK], BF16, name="w_bf", align_bytes=64)
-        def deal(copy, u, first, last):
+        for copy, first, last in ((nc.scalar.copy, 0, DEAL_SPLIT), (nc.vector.tensor_copy, DEAL_SPLIT, P)):
             copy(
-                w_bf[:, :, u * (P // 2) + first : u * (P // 2) + last, :].rearrange("p t m j -> p m j t"),
-                w_raw[u][:, :, PACK * first : PACK * last].rearrange("p j (m t) -> p m j t", t=PACK),
+                w_bf[:, :, first:last, :].rearrange("p t m j -> p m j t"),
+                w_raw[:, :, PACK * first : PACK * last].rearrange("p j (m t) -> p m j t", t=PACK),
             )
-
-        deal(nc.scalar.copy, 0, 0, P // 2)
-        deal(nc.scalar.copy, 1, 0, 24)
-        deal(nc.vector.tensor_copy, 1, 24, P // 2)
         w_c = keep.tile([P, H], U32, name="w_c", align_bytes=64)
         w_s = keep.tile([P, H], U8, name="w_s", align_bytes=64)
         for t in range(PACK):
@@ -128,8 +124,8 @@ def tile_picked_twocdmaxbmedgtan_none_p_kernel(
             nc.gpsimd.memset(tile[:, S:], 0.0)
             return tile
 
-        y2 = [window(f"y2_{t}", HALF * MEMBERS + SPARE) for t in range(PACK)]
-        y1 = [window(f"y1_{t}", 2 * S) for t in range(PACK)]
+        y2 = [window(f"y2_{t}", S + SPARE) for t in range(PACK)]
+        y1 = [keep.tile([P, S], F32, name=f"y1_{t}") for t in range(PACK)]
         a_sb, b_sb = y2, y1
         y1_bf = keep.tile([P, PACK, S], BF16, name="y1_bf")
         pa = keep.tile([P, PACK, S], BF16, name="pa")
@@ -142,15 +138,17 @@ def tile_picked_twocdmaxbmedgtan_none_p_kernel(
 
         def fetch_members(t, h):
             mb = ring.tile([P, HALF, MEMBERS], F32, name="mb", bufs=5)
-            lst = entries(n3_t, h * HALF * MEMBERS, HALF * MEMBERS)
-            nc.scalar.activation(mb[:].rearrange("p j m -> p (j m)"), y2[t][:].indirect(lst), ACT.Copy)
+            flat = mb[:].rearrange("p j m -> p (j m)")
+            for first in range(0, HALF * MEMBERS, S):
+                lst = entries(n3_t, h * HALF * MEMBERS + first, S)
+                nc.scalar.activation(flat[:, first : first + S], y2[t][:].indirect(lst), ACT.Copy)
             return mb
 
         def reduce_members(t, h, mb):
             big = ring.tile([P, HALF, 2], F32, name="big")
             small = ring.tile([P, HALF, 2], F32, name="small")
             mn = ring.tile([P, HALF], F32, name="mn")
-            diff = ring.tile([P, HALF], F32, name="diff", bufs=4)
+            diff = ring.tile([P, HALF], F32, name="diff", bufs=8)
             nc.vector.tensor_tensor(small[:], mb[:, :, 0:2], mb[:, :, 2:4], ALU.min)
             nc.vector.tensor_tensor(big[:], mb[:, :, 0:2], mb[:, :, 2:4], ALU.max)
             nc.vector.tensor_tensor(mn[:], small[:, :, 0], small[:, :, 1], ALU.min)
@@ -163,12 +161,17 @@ def tile_picked_twocdmaxbmedgtan_none_p_kernel(
 
         def weave_and_quantize(name, in0, in1, op, width):
             woven = keep.tile([P, width, PACK], BF16, name=f"{name}_bf", align_bytes=64)
-            nc.vector.tensor_tensor(
-                woven[:].rearrange("p (c i) t -> p c t i", i=LINE),
-                in0.rearrange("p t (c i) -> p c t i", i=LINE),
-                in1.rearrange("p t (c i) -> p c t i", i=LINE),
-                op,
-            )
+            if in1 is None:
+                nc.vector.tensor_copy(
+                    woven[:].rearrange("p (c i) t -> p c t i", i=LINE), in0.rearrange("p t (c i) -> p c t i", i=LINE)
+                )
+            else:
+                nc.vector.tensor_tensor(
+                    woven[:].rearrange("p (c i) t -> p c t i", i=LINE),
+                    in0.rearrange("p t (c i) -> p c t i", i=LINE),
+                    in1.rearrange("p t (c i) -> p c t i", i=LINE),
+                    op,
+                )
             codes = keep.tile([P, width], U32, name=f"{name}_c", align_bytes=64)
             scales = keep.tile([P, width], U8, name=f"{name}_s", align_bytes=64)
             nc.vector.quantize_mx(out=codes[:].bitcast(FP8X4), scales=scales[:], in_=woven[:].rearrange("p j t -> p (j t)"))
@@ -179,8 +182,10 @@ def tile_picked_twocdmaxbmedgtan_none_p_kernel(
             nc.vector.tensor_scalar(y1[t][:, :S], y_ps[t][:], g1[:, t : t + 1], None, ALU.mult)
         for t in range(PACK):
             (nc.scalar.copy if t < 1 else nc.vector.tensor_copy)(y1_bf[:, t, :], y1[t][:, :S])
-            nc.scalar.activation(pa[:, t, :], y1[t][:].indirect(n1_t[:]), ACT.Copy)
-            nc.vector.tensor_copy(pb[:, t, :], y1[t][:].indirect(n2_t[:]))
+            for first in (0, HALF):
+                cols = slice(first, first + HALF)
+                nc.scalar.activation(pa[:, t, cols], y1[t][:].indirect(entries(n1_t, first, HALF)), ACT.Copy)
+                nc.vector.tensor_copy(pb[:, t, cols], y1[t][:].indirect(entries(n2_t, first, HALF)))
         cb_s = pick_bytes("cb_s", cb_t, "w_bf")
         cb_w = pick_words("cb_w", cb_t, "words")
         for u in range(2):
@@ -188,6 +193,9 @@ def tile_picked_twocdmaxbmedgtan_none_p_kernel(
             nc.vector.tensor_tensor(hi[:, rows, :], y1_bf[:, rows, :], pa[:, rows, :], ALU.max)
             nc.vector.tensor_tensor(lo[:, rows, :], y1_bf[:, rows, :], pa[:, rows, :], ALU.min)
             nc.vector.tensor_tensor(mid[:, rows, :], hi[:, rows, :], pb[:, rows, :], ALU.min)
+        for u in range(2):
+            rows = slice(2 * u, 2 * u + 2)
+            nc.vector.tensor_tensor(hi[:, rows, :], lo[:, rows, :], mid[:, rows, :], ALU.max)
 
         a_ps = [psum.tile([P, S], F32, name=f"a_ps{c}", tag=f"a{c}") for c in range(PACK)]
         b_ps = [psum.tile([P, S], F32, name=f"b_ps{c}", tag=f"yb{c}") for c in range(PACK)]
@@ -204,7 +212,7 @@ def tile_picked_twocdmaxbmedgtan_none_p_kernel(
             nc.scalar.activation(a_sb[c][:, :S], a_ps[c][:], ACT.Copy, scale=0.0625)
             nc.scalar.activation(a4[:, c, :], a_sb[c][:].indirect(n4_t[:]), ACT.Copy)
 
-        z_c, z_s = weave_and_quantize("z", lo[:], mid[:], ALU.max, S)
+        z_c, z_s = weave_and_quantize("z", hi[:], None, None, S)
         for c in range(PACK):
             mx_product(a_ps[c][:], ca_w, ca_s, c, z_c[:], z_s[:])
         for h in range(2):
@@ -225,13 +233,14 @@ def tile_picked_twocdmaxbmedgtan_none_p_kernel(
         for c in range(PACK):
             if c > 0:
                 leave_b(c)
+            for first in (0, HALF):
+                nc.scalar.activation(b5[:, c, first : first + HALF], b_sb[c][:].indirect(entries(n5_t, first, HALF)), ACT.Copy)
             pieces = 2 if c == PACK - 1 else 1
             width = S // pieces
             for first in range(0, S, width):
                 cols = slice(first, first + width)
                 more = ring.tile([P, width], F32, name="more")
                 res = ring.tile([P, width], F32, name="res", bufs=5)
-                nc.scalar.activation(b5[:, c, cols], b_sb[c][:].indirect(entries(n5_t, first, width)), ACT.Copy)
                 nc.vector.tensor_tensor(more[:], a_sb[c][:, cols], b5[:, c, cols], ALU.max)
                 nc.vector.tensor_tensor(res[:], more[:], less[:, c, cols], ALU.subtract)
                 nc.sync.dma_start(out[P * c : P * (c + 1), cols], res[:])

@@ -63,6 +63,12 @@ def tile_picked_twocdmaxbmedgtan_none_p_kernel(
         n4_t = load_list("n4_t", n4)
         n5_t = load_list("n5_t", n5)
 
+        y2 = [keep.tile([P, S + SPARE], F32, name=f"y2_{t}") for t in range(PACK)]
+        for t in range(PACK):
+            nc.gpsimd.memset(y2[t][:, S:], 0.0)
+        warm = keep.tile([P, 1], F32, name="warm")
+        nc.scalar.activation(warm[:], y2[0][:, S : S + 1], ACT.Tanh)
+
         def pick_bytes(name, lst, tag):
             tile = keep.tile([P, S], U8, name=name, tag=tag, align_bytes=64)
             nc.vector.tensor_copy(tile[:], xs[:].indirect(lst[:]))
@@ -119,14 +125,8 @@ def tile_picked_twocdmaxbmedgtan_none_p_kernel(
         for t in range(PACK):
             mx_product(y_ps[t][:], w_c, w_s, t, xq_w[:], xq_s[:])
 
-        def window(name, width):
-            tile = keep.tile([P, width], F32, name=name)
-            nc.gpsimd.memset(tile[:, S:], 0.0)
-            return tile
-
-        y2 = [window(f"y2_{t}", S + SPARE) for t in range(PACK)]
         y1 = [keep.tile([P, S], F32, name=f"y1_{t}") for t in range(PACK)]
-        a_sb, b_sb = y2, y1
+        a_sb, b_sb = [y2[0], y2[1], y2[3], y2[2]], y1
         y1_bf = keep.tile([P, PACK, S], BF16, name="y1_bf")
         pa = keep.tile([P, PACK, S], BF16, name="pa")
         pb = keep.tile([P, PACK, S], BF16, name="pb")
@@ -181,7 +181,7 @@ def tile_picked_twocdmaxbmedgtan_none_p_kernel(
             nc.scalar.activation(y2[t][:, :S], y_ps[t][:], ACT.Copy, scale=g2_abs[:, t : t + 1])
             nc.vector.tensor_scalar(y1[t][:, :S], y_ps[t][:], g1[:, t : t + 1], None, ALU.mult)
         for t in range(PACK):
-            (nc.scalar.copy if t < 1 else nc.vector.tensor_copy)(y1_bf[:, t, :], y1[t][:, :S])
+            (nc.scalar.copy if t < 3 else nc.vector.tensor_copy)(y1_bf[:, t, :], y1[t][:, :S])
             for first in (0, HALF):
                 cols = slice(first, first + HALF)
                 nc.scalar.activation(pa[:, t, cols], y1[t][:].indirect(entries(n1_t, first, HALF)), ACT.Copy)
@@ -199,7 +199,7 @@ def tile_picked_twocdmaxbmedgtan_none_p_kernel(
 
         a_ps = [psum.tile([P, S], F32, name=f"a_ps{c}", tag=f"a{c}") for c in range(PACK)]
         b_ps = [psum.tile([P, S], F32, name=f"b_ps{c}", tag=f"yb{c}") for c in range(PACK)]
-        a4 = keep.tile([P, PACK, S], F32, name="a4")
+        a4 = {}
         b5 = keep.tile([P, PACK, S], F32, name="b5")
         less = keep.tile([P, PACK, S], F32, name="less")
 
@@ -209,8 +209,15 @@ def tile_picked_twocdmaxbmedgtan_none_p_kernel(
                 mx_product(b_ps[c][:, h * HALF : (h + 1) * HALF], cb_w, cb_s, c, z2_c[:], z2_s[:])
 
         def leave_and_fetch_a(c):
-            nc.scalar.activation(a_sb[c][:, :S], a_ps[c][:], ACT.Copy, scale=0.0625)
-            nc.scalar.activation(a4[:, c, :], a_sb[c][:].indirect(n4_t[:]), ACT.Copy)
+            if c < PACK - 1:
+                a4[c] = keep.tile([P, S], F32, name=f"a4_{c}")
+                nc.scalar.activation(a_sb[c][:, :S], a_ps[c][:], ACT.Copy, scale=0.0625)
+                nc.scalar.activation(a4[c][:], a_sb[c][:].indirect(n4_t[:]), ACT.Copy)
+            else:
+                a4[c] = keep.tile([P, S], F32, name=f"a4_{c}", tag="z2_1_bf", align_bytes=64)
+                nc.vector.tensor_scalar(a_sb[c][:, :S], a_ps[c][:], 0.0625, None, ALU.mult)
+                for first in (0, HALF):
+                    nc.vector.tensor_copy(a4[c][:, first : first + HALF], a_sb[c][:].indirect(entries(n4_t, first, HALF)))
 
         z_c, z_s = weave_and_quantize("z", hi[:], None, None, S)
         for c in range(PACK):
@@ -225,22 +232,23 @@ def tile_picked_twocdmaxbmedgtan_none_p_kernel(
             leave_and_fetch_a(c)
 
         def leave_b(c):
-            nc.scalar.activation(b_sb[c][:, :S], b_ps[c][:], ACT.Copy, scale=0.0625)
+            if c < PACK - 2:
+                nc.scalar.activation(b_sb[c][:, :S], b_ps[c][:], ACT.Copy, scale=0.0625)
+            else:
+                nc.vector.tensor_scalar(b_sb[c][:, :S], b_ps[c][:], 0.0625, None, ALU.mult)
 
-        leave_b(0)
-        for c in (1, 2, 0, 3):
-            nc.vector.scalar_tensor_tensor(less[:, c, :], b_ps[c][:], 0.0625, a4[:, c, :], ALU.mult, ALU.min)
         for c in range(PACK):
-            if c > 0:
-                leave_b(c)
+            leave_b(c)
+        for c in range(PACK):
             for first in (0, HALF):
                 nc.scalar.activation(b5[:, c, first : first + HALF], b_sb[c][:].indirect(entries(n5_t, first, HALF)), ACT.Copy)
+            nc.vector.scalar_tensor_tensor(less[:, c, :], b_ps[c][:], 0.0625, a4[c][:], ALU.mult, ALU.min)
             pieces = 2 if c == PACK - 1 else 1
             width = S // pieces
             for first in range(0, S, width):
                 cols = slice(first, first + width)
-                more = ring.tile([P, width], F32, name="more")
+                more = ring.tile([P, width], F32, name="more", bufs=5)
                 res = ring.tile([P, width], F32, name="res", bufs=5)
-                nc.vector.tensor_tensor(more[:], a_sb[c][:, cols], b5[:, c, cols], ALU.max)
-                nc.vector.tensor_tensor(res[:], more[:], less[:, c, cols], ALU.subtract)
+                nc.vector.scalar_tensor_tensor(more[:], a_ps[c][:, cols], 0.0625, b5[:, c, cols], ALU.mult, ALU.max)
+                (nc.gpsimd if c < 3 else nc.vector).tensor_tensor(res[:], more[:], less[:, c, cols], ALU.subtract)
                 nc.sync.dma_start(out[P * c : P * (c + 1), cols], res[:])

@@ -2,7 +2,7 @@ from contextlib import ExitStack
 
 import concourse.mybir as mybir
 
-K, T, S, H, C = 512, 2048, 512, 512, 512
+T, S, H = 2048, 512, 512
 FLOPS = 3 * 2 * 512 * 512 * 512
 
 F32 = mybir.dt.float32
@@ -17,12 +17,19 @@ ACT = mybir.ActivationFunctionType
 
 P = 128
 PACK = 4
+LAST = PACK - 1
 HALF = S // 2
 MEMBERS = 4
 SPARE = 16
 LINE = 4
-LATE = 2
-DEAL_SPLIT = 40
+SIXTEENTH = 0.0625
+SMALLEST_NORMAL = 2.0**-126
+
+W_COLUMNS_ON_SCALAR = 56
+PB_TILES_ON_VECTOR = 3
+B_TILES_ON_SCALAR = 2
+FIRST_HALF_SCORED_AFTER = 2
+MEMBER_BUFFERS = 5
 
 
 def tile_picked_twocdmaxbmedgtan_none_p_kernel(
@@ -41,6 +48,18 @@ def tile_picked_twocdmaxbmedgtan_none_p_kernel(
 
         def entries(tile, first, count):
             return tile[:, first // 16 : (first + count) // 16]
+
+        def gather(engine, dst, window, offsets):
+            if engine == "scalar":
+                nc.scalar.activation(dst, window.indirect(offsets), ACT.Copy)
+            else:
+                nc.vector.tensor_copy(dst, window.indirect(offsets))
+
+        def leave_bank(engine, dst, bank, factor):
+            if engine == "scalar":
+                nc.scalar.activation(dst, bank, ACT.Copy, scale=factor)
+            else:
+                nc.vector.tensor_scalar(dst, bank, factor, None, ALU.mult)
 
         xs = keep.tile([P, T], U8, name="xs", align_bytes=64)
         nc.gpsimd.memset(xs[:].bitcast(I32), 0)
@@ -63,51 +82,57 @@ def tile_picked_twocdmaxbmedgtan_none_p_kernel(
         n4_t = load_list("n4_t", n4)
         n5_t = load_list("n5_t", n5)
 
-        y2 = [keep.tile([P, S + SPARE], F32, name=f"y2_{t}") for t in range(PACK)]
+        y2 = [keep.tile([P, HALF * MEMBERS + SPARE], F32, name=f"y2_{t}") for t in range(PACK)]
         for t in range(PACK):
-            nc.gpsimd.memset(y2[t][:, S:], 0.0)
+            nc.vector.memset(y2[t][:, S:], 0.0)
         warm = keep.tile([P, 1], F32, name="warm")
         nc.scalar.activation(warm[:], y2[0][:, S : S + 1], ACT.Tanh)
 
         def pick_bytes(name, lst, tag):
             tile = keep.tile([P, S], U8, name=name, tag=tag, align_bytes=64)
-            nc.vector.tensor_copy(tile[:], xs[:].indirect(lst[:]))
+            gather("vector", tile[:], xs[:], lst[:])
             return tile
 
         def pick_words(name, lst, tag):
             tile = keep.tile([P, S], U32, name=name, tag=tag, align_bytes=64)
-            nc.vector.tensor_copy(tile[:], xw[:].bitcast(U32).indirect(lst[:]))
+            gather("vector", tile[:], xw[:].bitcast(U32), lst[:])
             return tile
 
         xq_s = pick_bytes("xq_s", offs_t, "xq_s")
         ca_s = pick_bytes("ca_s", ca_t, "ca_s")
+
         g2_neg = keep.tile([P, PACK], F32, name="g2_neg")
         g2_abs = keep.tile([P, PACK], F32, name="g2_abs")
         g2_floor = keep.tile([P, PACK], F32, name="g2_floor")
         g2_rec = keep.tile([P, PACK], F32, name="g2_rec")
-        g2_sign = keep.tile([P, PACK], F32, name="g2_sign")
+        g2_step = keep.tile([P, PACK], F32, name="g2_step")
         g2_inv = keep.tile([P, PACK], F32, name="g2_inv")
         nc.vector.tensor_scalar(g2_neg[:], g2[:], -1.0, None, ALU.mult)
-        nc.vector.tensor_scalar(g2_sign[:], g2[:], 0.0, 2.0, ALU.is_ge, ALU.mult)
+        nc.vector.tensor_scalar(g2_step[:], g2[:], 0.0, 2.0, ALU.is_ge, ALU.mult)
         nc.vector.tensor_tensor(g2_abs[:], g2[:], g2_neg[:], ALU.max)
-        nc.vector.tensor_scalar(g2_floor[:], g2_abs[:], 2.0**-126, None, ALU.max)
+        nc.vector.tensor_scalar(g2_floor[:], g2_abs[:], SMALLEST_NORMAL, None, ALU.max)
         nc.vector.reciprocal(g2_rec[:], g2_floor[:])
-        nc.vector.scalar_tensor_tensor(g2_inv[:], g2_sign[:], -1.0, g2_rec[:], ALU.add, ALU.mult)
+        nc.vector.scalar_tensor_tensor(g2_inv[:], g2_step[:], -1.0, g2_rec[:], ALU.add, ALU.mult)
 
-        xq_w = pick_words("xq_w", offs_t, "words")
+        xq_w = pick_words("xq_w", offs_t, "moving_words")
         ca_w = pick_words("ca_w", ca_t, "ca_w")
 
         w_bf = keep.tile([P, PACK, P, PACK], BF16, name="w_bf", align_bytes=64)
-        for copy, first, last in ((nc.scalar.copy, 0, DEAL_SPLIT), (nc.vector.tensor_copy, DEAL_SPLIT, P)):
+        for copy, first, end in (
+            (nc.scalar.copy, 0, W_COLUMNS_ON_SCALAR),
+            (nc.vector.tensor_copy, W_COLUMNS_ON_SCALAR, P),
+        ):
             copy(
-                w_bf[:, :, first:last, :].rearrange("p t m j -> p m j t"),
-                w_raw[:, :, PACK * first : PACK * last].rearrange("p j (m t) -> p m j t", t=PACK),
+                w_bf[:, :, first:end, :].rearrange("p t m j -> p m j t"),
+                w_raw[:, :, PACK * first : PACK * end].rearrange("p j (m t) -> p m j t", t=PACK),
             )
         w_c = keep.tile([P, H], U32, name="w_c", align_bytes=64)
         w_s = keep.tile([P, H], U8, name="w_s", align_bytes=64)
         for t in range(PACK):
             cols = slice(P * t, P * (t + 1))
-            nc.vector.quantize_mx(out=w_c[:, cols].bitcast(FP8X4), scales=w_s[:, cols], in_=w_bf[:, t].rearrange("p m j -> p (m j)"))
+            nc.vector.quantize_mx(
+                out=w_c[:, cols].bitcast(FP8X4), scales=w_s[:, cols], in_=w_bf[:, t].rearrange("p m j -> p (m j)")
+            )
 
         def mx_product(bank, lhs_w, lhs_s, tile_no, rhs_w, rhs_s):
             cols = slice(P * tile_no, P * (tile_no + 1))
@@ -121,134 +146,112 @@ def tile_picked_twocdmaxbmedgtan_none_p_kernel(
                 stop=True,
             )
 
-        y_ps = [psum.tile([P, S], F32, name=f"y_ps{t}", tag=f"yb{t}") for t in range(PACK)]
+        y_ps = [psum.tile([P, S], F32, name=f"y_ps{t}", tag=f"y_then_b{t}") for t in range(PACK)]
         for t in range(PACK):
             mx_product(y_ps[t][:], w_c, w_s, t, xq_w[:], xq_s[:])
 
+        def interleaved(rows):
+            return rows.rearrange("p t (c i) -> p c t i", i=LINE)
+
+        def packed_tile(name, width):
+            tile = keep.tile([P, width, PACK], BF16, name=name, align_bytes=64)
+            return tile, tile[:].rearrange("p (c i) t -> p c t i", i=LINE)
+
+        def quantize(name, tile, width):
+            codes = keep.tile([P, width], U32, name=f"{name}_c", align_bytes=64)
+            scales = keep.tile([P, width], U8, name=f"{name}_s", align_bytes=64)
+            nc.vector.quantize_mx(out=codes[:].bitcast(FP8X4), scales=scales[:], in_=tile[:].rearrange("p j t -> p (j t)"))
+            return codes, scales
+
         y1 = [keep.tile([P, S], F32, name=f"y1_{t}") for t in range(PACK)]
-        a_sb, b_sb = [y2[0], y2[1], y2[3], y2[2]], y1
         y1_bf = keep.tile([P, PACK, S], BF16, name="y1_bf")
         pa = keep.tile([P, PACK, S], BF16, name="pa")
         pb = keep.tile([P, PACK, S], BF16, name="pb")
         lo = keep.tile([P, PACK, S], BF16, name="lo")
         hi = keep.tile([P, PACK, S], BF16, name="hi")
         mid = keep.tile([P, PACK, S], BF16, name="mid")
+        for t in range(PACK):
+            leave_bank("scalar", y2[t][:, :S], y_ps[t][:], g2_abs[:, t : t + 1])
+            leave_bank("vector", y1[t][:], y_ps[t][:], g1[:, t : t + 1])
+        for t in range(PACK):
+            nc.gpsimd.tensor_scalar(y1_bf[:, t, :], y1[t][:], 1.0, 0.0, ALU.mult, ALU.add)
+            for first in (0, HALF):
+                cols = slice(first, first + HALF)
+                gather("scalar", pa[:, t, cols], y1[t][:], entries(n1_t, first, HALF))
+                gather("vector" if t < PB_TILES_ON_VECTOR else "scalar", pb[:, t, cols], y1[t][:], entries(n2_t, first, HALF))
+        cb_s = pick_bytes("cb_s", cb_t, "w_bf")
+        cb_w = pick_words("cb_w", cb_t, "moving_words")
+        pairs = (slice(0, 2), slice(2, 4))
+        for rows in pairs:
+            nc.vector.tensor_tensor(hi[:, rows, :], y1_bf[:, rows, :], pa[:, rows, :], ALU.max)
+            nc.vector.tensor_tensor(lo[:, rows, :], y1_bf[:, rows, :], pa[:, rows, :], ALU.min)
+            nc.vector.tensor_tensor(mid[:, rows, :], hi[:, rows, :], pb[:, rows, :], ALU.min)
+        z_rows = hi
+        for rows in pairs:
+            nc.vector.tensor_tensor(z_rows[:, rows, :], lo[:, rows, :], mid[:, rows, :], ALU.max)
+        z_bf, z_walk = packed_tile("z_bf", S)
+        nc.vector.tensor_copy(z_walk, interleaved(z_rows[:]))
+        z_c, z_s = quantize("z", z_bf, S)
+        a_ps = [psum.tile([P, S], F32, name=f"a_ps{c}", tag=f"a{c}") for c in range(PACK)]
+        for c in range(PACK):
+            mx_product(a_ps[c][:], ca_w, ca_s, c, z_c[:], z_s[:])
+
         mx = [keep.tile([P, PACK, HALF], F32, name=f"mx{h}") for h in range(2)]
         th = [keep.tile([P, PACK, HALF], F32, name=f"th{h}") for h in range(2)]
+        b_ps = [psum.tile([P, S], F32, name=f"b_ps{c}", tag=f"y_then_b{c}") for c in range(PACK)]
 
-        def fetch_members(t, h):
-            mb = ring.tile([P, HALF, MEMBERS], F32, name="mb", bufs=5)
-            flat = mb[:].rearrange("p j m -> p (j m)")
-            for first in range(0, HALF * MEMBERS, S):
-                lst = entries(n3_t, h * HALF * MEMBERS + first, S)
-                nc.scalar.activation(flat[:, first : first + S], y2[t][:].indirect(lst), ACT.Copy)
-            return mb
-
-        def reduce_members(t, h, mb):
+        def largest_and_tanh(t, h):
+            mb = ring.tile([P, HALF, MEMBERS], F32, name="mb", bufs=MEMBER_BUFFERS)
+            gather("scalar", mb[:].rearrange("p j m -> p (j m)"), y2[t][:], entries(n3_t, h * HALF * MEMBERS, HALF * MEMBERS))
             big = ring.tile([P, HALF, 2], F32, name="big")
             small = ring.tile([P, HALF, 2], F32, name="small")
             mn = ring.tile([P, HALF], F32, name="mn")
-            diff = ring.tile([P, HALF], F32, name="diff", bufs=8)
+            diff = ring.tile([P, HALF], F32, name="diff", bufs=2 * PACK)
             nc.vector.tensor_tensor(small[:], mb[:, :, 0:2], mb[:, :, 2:4], ALU.min)
             nc.vector.tensor_tensor(big[:], mb[:, :, 0:2], mb[:, :, 2:4], ALU.max)
             nc.vector.tensor_tensor(mn[:], small[:, :, 0], small[:, :, 1], ALU.min)
             nc.vector.tensor_tensor(mx[h][:, t, :], big[:, :, 0], big[:, :, 1], ALU.max)
             nc.vector.tensor_tensor(diff[:], y2[t][:, h * HALF : (h + 1) * HALF], mn[:], ALU.subtract)
-            return diff
-
-        def squash(t, h, diff):
             nc.scalar.activation(th[h][:, t, :], diff[:], ACT.Tanh, scale=g2_inv[:, t : t + 1])
 
-        def weave_and_quantize(name, in0, in1, op, width):
-            woven = keep.tile([P, width, PACK], BF16, name=f"{name}_bf", align_bytes=64)
-            if in1 is None:
-                nc.vector.tensor_copy(
-                    woven[:].rearrange("p (c i) t -> p c t i", i=LINE), in0.rearrange("p t (c i) -> p c t i", i=LINE)
-                )
-            else:
-                nc.vector.tensor_tensor(
-                    woven[:].rearrange("p (c i) t -> p c t i", i=LINE),
-                    in0.rearrange("p t (c i) -> p c t i", i=LINE),
-                    in1.rearrange("p t (c i) -> p c t i", i=LINE),
-                    op,
-                )
-            codes = keep.tile([P, width], U32, name=f"{name}_c", align_bytes=64)
-            scales = keep.tile([P, width], U8, name=f"{name}_s", align_bytes=64)
-            nc.vector.quantize_mx(out=codes[:].bitcast(FP8X4), scales=scales[:], in_=woven[:].rearrange("p j t -> p (j t)"))
-            return codes, scales
-
-        for t in range(PACK):
-            nc.scalar.activation(y2[t][:, :S], y_ps[t][:], ACT.Copy, scale=g2_abs[:, t : t + 1])
-            nc.vector.tensor_scalar(y1[t][:, :S], y_ps[t][:], g1[:, t : t + 1], None, ALU.mult)
-        for t in range(PACK):
-            (nc.scalar.copy if t < 3 else nc.vector.tensor_copy)(y1_bf[:, t, :], y1[t][:, :S])
-            for first in (0, HALF):
-                cols = slice(first, first + HALF)
-                nc.scalar.activation(pa[:, t, cols], y1[t][:].indirect(entries(n1_t, first, HALF)), ACT.Copy)
-                nc.vector.tensor_copy(pb[:, t, cols], y1[t][:].indirect(entries(n2_t, first, HALF)))
-        cb_s = pick_bytes("cb_s", cb_t, "w_bf")
-        cb_w = pick_words("cb_w", cb_t, "words")
-        for u in range(2):
-            rows = slice(2 * u, 2 * u + 2)
-            nc.vector.tensor_tensor(hi[:, rows, :], y1_bf[:, rows, :], pa[:, rows, :], ALU.max)
-            nc.vector.tensor_tensor(lo[:, rows, :], y1_bf[:, rows, :], pa[:, rows, :], ALU.min)
-            nc.vector.tensor_tensor(mid[:, rows, :], hi[:, rows, :], pb[:, rows, :], ALU.min)
-        for u in range(2):
-            rows = slice(2 * u, 2 * u + 2)
-            nc.vector.tensor_tensor(hi[:, rows, :], lo[:, rows, :], mid[:, rows, :], ALU.max)
-
-        a_ps = [psum.tile([P, S], F32, name=f"a_ps{c}", tag=f"a{c}") for c in range(PACK)]
-        b_ps = [psum.tile([P, S], F32, name=f"b_ps{c}", tag=f"yb{c}") for c in range(PACK)]
-        a4 = {}
-        b5 = keep.tile([P, PACK, S], F32, name="b5")
-        less = keep.tile([P, PACK, S], F32, name="less")
-
-        def score_b(h):
-            z2_c, z2_s = weave_and_quantize(f"z2_{h}", mx[h][:], th[h][:], ALU.mult, HALF)
+        def score_half(h):
+            z2_bf, z2_walk = packed_tile(f"z2_{h}_bf", HALF)
+            nc.vector.tensor_tensor(z2_walk, interleaved(mx[h][:]), interleaved(th[h][:]), ALU.mult)
+            z2_c, z2_s = quantize(f"z2_{h}", z2_bf, HALF)
             for c in range(PACK):
                 mx_product(b_ps[c][:, h * HALF : (h + 1) * HALF], cb_w, cb_s, c, z2_c[:], z2_s[:])
 
-        def leave_and_fetch_a(c):
-            if c < PACK - 1:
-                a4[c] = keep.tile([P, S], F32, name=f"a4_{c}")
-                nc.scalar.activation(a_sb[c][:, :S], a_ps[c][:], ACT.Copy, scale=0.0625)
-                nc.scalar.activation(a4[c][:], a_sb[c][:].indirect(n4_t[:]), ACT.Copy)
-            else:
-                a4[c] = keep.tile([P, S], F32, name=f"a4_{c}", tag="z2_1_bf", align_bytes=64)
-                nc.vector.tensor_scalar(a_sb[c][:, :S], a_ps[c][:], 0.0625, None, ALU.mult)
-                for first in (0, HALF):
-                    nc.vector.tensor_copy(a4[c][:, first : first + HALF], a_sb[c][:].indirect(entries(n4_t, first, HALF)))
-
-        z_c, z_s = weave_and_quantize("z", hi[:], None, None, S)
-        for c in range(PACK):
-            mx_product(a_ps[c][:], ca_w, ca_s, c, z_c[:], z_s[:])
         for h in range(2):
             for t in range(PACK):
-                squash(t, h, reduce_members(t, h, fetch_members(t, h)))
-                if (h, t) == (1, LATE):
-                    score_b(0)
-        score_b(1)
-        for c in range(PACK):
-            leave_and_fetch_a(c)
+                largest_and_tanh(t, h)
+                if (h, t) == (1, FIRST_HALF_SCORED_AFTER):
+                    score_half(0)
+        score_half(1)
 
-        def leave_b(c):
-            if c < PACK - 2:
-                nc.scalar.activation(b_sb[c][:, :S], b_ps[c][:], ACT.Copy, scale=0.0625)
-            else:
-                nc.vector.tensor_scalar(b_sb[c][:, :S], b_ps[c][:], 0.0625, None, ALU.mult)
-
+        a_sb = [y2[0], y2[1], y2[3], y2[2]]
+        a4 = []
         for c in range(PACK):
-            leave_b(c)
+            engine = "scalar" if c < LAST else "vector"
+            fetched = keep.tile([P, S], F32, name=f"a4_{c}", tag=f"a4_{c}" if c < LAST else "z2_1_bf", align_bytes=64)
+            leave_bank(engine, a_sb[c][:, :S], a_ps[c][:], SIXTEENTH)
+            gather(engine, fetched[:], a_sb[c][:], n4_t[:])
+            a4.append(fetched)
+
+        b_sb = y1
+        b5 = keep.tile([P, PACK, S], F32, name="b5")
+        less = keep.tile([P, PACK, S], F32, name="less")
+        for c in range(PACK):
+            leave_bank("scalar" if c < B_TILES_ON_SCALAR else "vector", b_sb[c][:], b_ps[c][:], SIXTEENTH)
         for c in range(PACK):
             for first in (0, HALF):
-                nc.scalar.activation(b5[:, c, first : first + HALF], b_sb[c][:].indirect(entries(n5_t, first, HALF)), ACT.Copy)
-            nc.vector.scalar_tensor_tensor(less[:, c, :], b_ps[c][:], 0.0625, a4[c][:], ALU.mult, ALU.min)
-            pieces = 2 if c == PACK - 1 else 1
-            width = S // pieces
+                gather("scalar", b5[:, c, first : first + HALF], b_sb[c][:], entries(n5_t, first, HALF))
+            nc.vector.scalar_tensor_tensor(less[:, c, :], b_ps[c][:], SIXTEENTH, a4[c][:], ALU.mult, ALU.min)
+            width = S if c < LAST else HALF
+            subtractor = nc.gpsimd if c < LAST else nc.vector
             for first in range(0, S, width):
                 cols = slice(first, first + width)
-                more = ring.tile([P, width], F32, name="more", bufs=5)
-                res = ring.tile([P, width], F32, name="res", bufs=5)
-                nc.vector.scalar_tensor_tensor(more[:], a_ps[c][:, cols], 0.0625, b5[:, c, cols], ALU.mult, ALU.max)
-                (nc.gpsimd if c < 3 else nc.vector).tensor_tensor(res[:], more[:], less[:, c, cols], ALU.subtract)
+                more = ring.tile([P, width], F32, name="more", bufs=PACK + 1)
+                res = ring.tile([P, width], F32, name="res", bufs=PACK + 1)
+                nc.vector.scalar_tensor_tensor(more[:], a_ps[c][:, cols], SIXTEENTH, b5[:, c, cols], ALU.mult, ALU.max)
+                subtractor.tensor_tensor(res[:], more[:], less[:, c, cols], ALU.subtract)
                 nc.sync.dma_start(out[P * c : P * (c + 1), cols], res[:])

from contextlib import ExitStack

import concourse.mybir as mybir

T, S, H = 2048, 512, 512
FLOPS = 3 * 2 * 512 * 512 * 512

F32 = mybir.dt.float32
BF16 = mybir.dt.bfloat16
I32 = mybir.dt.int32
U32 = mybir.dt.uint32
U16 = mybir.dt.uint16
U8 = mybir.dt.uint8
FP8X4 = mybir.dt.float8_e4m3fn_x4
ALU = mybir.AluOpType
ACT = mybir.ActivationFunctionType

P = 128
PACK = 4
LAST = PACK - 1
HALF = S // 2
MEMBERS = 4
SPARE = 16
LINE = 4
SIXTEENTH = 0.0625
SMALLEST_NORMAL = 2.0**-126

W_COLUMNS_ON_SCALAR = 56
PB_TILES_ON_VECTOR = 3
B_TILES_ON_SCALAR = 2
FIRST_HALF_SCORED_AFTER = 2
MEMBER_BUFFERS = 5


def tile_picked_twocdmaxbmedgtan_none_p_kernel(
    tc, x_words, x_scales, w1, gs, gs2, offs, n1, n2, n3, ca, cb, n4, n5, out
):
    nc = tc.nc
    with ExitStack() as ctx:
        keep = ctx.enter_context(tc.tile_pool(name="keep", bufs=1))
        ring = ctx.enter_context(tc.tile_pool(name="ring", bufs=2))
        psum = ctx.enter_context(tc.psum_pool(name="psum", bufs=1))

        def load_list(name, src):
            tile = keep.tile(list(src.shape), U16, name=name)
            nc.sync.dma_start(tile[:], src)
            return tile

        def entries(tile, first, count):
            return tile[:, first // 16 : (first + count) // 16]

        def gather(engine, dst, window, offsets):
            if engine == "scalar":
                nc.scalar.activation(dst, window.indirect(offsets), ACT.Copy)
            else:
                nc.vector.tensor_copy(dst, window.indirect(offsets))

        def leave_bank(engine, dst, bank, factor):
            if engine == "scalar":
                nc.scalar.activation(dst, bank, ACT.Copy, scale=factor)
            else:
                nc.vector.tensor_scalar(dst, bank, factor, None, ALU.mult)

        xs = keep.tile([P, T], U8, name="xs", align_bytes=64)
        nc.gpsimd.memset(xs[:].bitcast(I32), 0)
        offs_t = load_list("offs_t", offs)
        ca_t = load_list("ca_t", ca)
        g2 = keep.tile([P, PACK], F32, name="g2")
        nc.sync.dma_start(g2[:], gs2.rearrange("(p t) o -> p (t o)", t=PACK))
        for q in range(4):
            nc.sync.dma_start(xs[32 * q : 32 * q + 4, :].bitcast(I32), x_scales[0, 4 * q : 4 * q + 4, :].bitcast(I32))
        xw = keep.tile([P, T], I32, name="xw", align_bytes=64)
        nc.sync.dma_start(xw[:], x_words[0].rearrange("p n t -> p (n t)").bitcast(I32))
        w_raw = keep.tile([P, PACK, H], F32, name="w_raw")
        nc.sync.dma_start(w_raw[:], w1.rearrange("(p j) c -> p j c", j=PACK))
        n3_t = load_list("n3_t", n3)
        g1 = keep.tile([P, PACK], F32, name="g1")
        nc.sync.dma_start(g1[:], gs.rearrange("(p t) o -> p (t o)", t=PACK))
        n2_t = load_list("n2_t", n2)
        n1_t = load_list("n1_t", n1)
        cb_t = load_list("cb_t", cb)
        n4_t = load_list("n4_t", n4)
        n5_t = load_list("n5_t", n5)

        y2 = [keep.tile([P, HALF * MEMBERS + SPARE], F32, name=f"y2_{t}") for t in range(PACK)]
        for t in range(PACK):
            nc.vector.memset(y2[t][:, S:], 0.0)
        warm = keep.tile([P, 1], F32, name="warm")
        nc.scalar.activation(warm[:], y2[0][:, S : S + 1], ACT.Tanh)

        def pick_bytes(name, lst, tag):
            tile = keep.tile([P, S], U8, name=name, tag=tag, align_bytes=64)
            gather("vector", tile[:], xs[:], lst[:])
            return tile

        def pick_words(name, lst, tag):
            tile = keep.tile([P, S], U32, name=name, tag=tag, align_bytes=64)
            gather("vector", tile[:], xw[:].bitcast(U32), lst[:])
            return tile

        xq_s = pick_bytes("xq_s", offs_t, "xq_s")
        ca_s = pick_bytes("ca_s", ca_t, "ca_s")

        g2_neg = keep.tile([P, PACK], F32, name="g2_neg")
        g2_abs = keep.tile([P, PACK], F32, name="g2_abs")
        g2_floor = keep.tile([P, PACK], F32, name="g2_floor")
        g2_rec = keep.tile([P, PACK], F32, name="g2_rec")
        g2_step = keep.tile([P, PACK], F32, name="g2_step")
        g2_inv = keep.tile([P, PACK], F32, name="g2_inv")
        nc.vector.tensor_scalar(g2_neg[:], g2[:], -1.0, None, ALU.mult)
        nc.vector.tensor_scalar(g2_step[:], g2[:], 0.0, 2.0, ALU.is_ge, ALU.mult)
        nc.vector.tensor_tensor(g2_abs[:], g2[:], g2_neg[:], ALU.max)
        nc.vector.tensor_scalar(g2_floor[:], g2_abs[:], SMALLEST_NORMAL, None, ALU.max)
        nc.vector.reciprocal(g2_rec[:], g2_floor[:])
        nc.vector.scalar_tensor_tensor(g2_inv[:], g2_step[:], -1.0, g2_rec[:], ALU.add, ALU.mult)

        xq_w = pick_words("xq_w", offs_t, "moving_words")
        ca_w = pick_words("ca_w", ca_t, "ca_w")

        w_bf = keep.tile([P, PACK, P, PACK], BF16, name="w_bf", align_bytes=64)
        for copy, first, end in (
            (nc.scalar.copy, 0, W_COLUMNS_ON_SCALAR),
            (nc.vector.tensor_copy, W_COLUMNS_ON_SCALAR, P),
        ):
            copy(
                w_bf[:, :, first:end, :].rearrange("p t m j -> p m j t"),
                w_raw[:, :, PACK * first : PACK * end].rearrange("p j (m t) -> p m j t", t=PACK),
            )
        w_c = keep.tile([P, H], U32, name="w_c", align_bytes=64)
        w_s = keep.tile([P, H], U8, name="w_s", align_bytes=64)
        for t in range(PACK):
            cols = slice(P * t, P * (t + 1))
            nc.vector.quantize_mx(
                out=w_c[:, cols].bitcast(FP8X4), scales=w_s[:, cols], in_=w_bf[:, t].rearrange("p m j -> p (m j)")
            )

        def mx_product(bank, lhs_w, lhs_s, tile_no, rhs_w, rhs_s):
            cols = slice(P * tile_no, P * (tile_no + 1))
            nc.tensor.matmul_mx(
                out=bank,
                lhsT=lhs_w[:, cols].bitcast(FP8X4),
                lhsT_scale=lhs_s[:, cols],
                rhs=rhs_w.bitcast(FP8X4),
                rhs_scale=rhs_s,
                start=True,
                stop=True,
            )

        y_ps = [psum.tile([P, S], F32, name=f"y_ps{t}", tag=f"y_then_b{t}") for t in range(PACK)]
        for t in range(PACK):
            mx_product(y_ps[t][:], w_c, w_s, t, xq_w[:], xq_s[:])

        def interleaved(rows):
            return rows.rearrange("p t (c i) -> p c t i", i=LINE)

        def packed_tile(name, width):
            tile = keep.tile([P, width, PACK], BF16, name=name, align_bytes=64)
            return tile, tile[:].rearrange("p (c i) t -> p c t i", i=LINE)

        def quantize(name, tile, width):
            codes = keep.tile([P, width], U32, name=f"{name}_c", align_bytes=64)
            scales = keep.tile([P, width], U8, name=f"{name}_s", align_bytes=64)
            nc.vector.quantize_mx(out=codes[:].bitcast(FP8X4), scales=scales[:], in_=tile[:].rearrange("p j t -> p (j t)"))
            return codes, scales

        y1 = [keep.tile([P, S], F32, name=f"y1_{t}") for t in range(PACK)]
        y1_bf = keep.tile([P, PACK, S], BF16, name="y1_bf")
        pa = keep.tile([P, PACK, S], BF16, name="pa")
        pb = keep.tile([P, PACK, S], BF16, name="pb")
        lo = keep.tile([P, PACK, S], BF16, name="lo")
        hi = keep.tile([P, PACK, S], BF16, name="hi")
        mid = keep.tile([P, PACK, S], BF16, name="mid")
        for t in range(PACK):
            leave_bank("scalar", y2[t][:, :S], y_ps[t][:], g2_abs[:, t : t + 1])
            leave_bank("vector", y1[t][:], y_ps[t][:], g1[:, t : t + 1])
        for t in range(PACK):
            nc.gpsimd.tensor_scalar(y1_bf[:, t, :], y1[t][:], 1.0, 0.0, ALU.mult, ALU.add)
            for first in (0, HALF):
                cols = slice(first, first + HALF)
                gather("scalar", pa[:, t, cols], y1[t][:], entries(n1_t, first, HALF))
                gather("vector" if t < PB_TILES_ON_VECTOR else "scalar", pb[:, t, cols], y1[t][:], entries(n2_t, first, HALF))
        cb_s = pick_bytes("cb_s", cb_t, "w_bf")
        cb_w = pick_words("cb_w", cb_t, "moving_words")
        pairs = (slice(0, 2), slice(2, 4))
        for rows in pairs:
            nc.vector.tensor_tensor(hi[:, rows, :], y1_bf[:, rows, :], pa[:, rows, :], ALU.max)
            nc.vector.tensor_tensor(lo[:, rows, :], y1_bf[:, rows, :], pa[:, rows, :], ALU.min)
            nc.vector.tensor_tensor(mid[:, rows, :], hi[:, rows, :], pb[:, rows, :], ALU.min)
        z_rows = hi
        for rows in pairs:
            nc.vector.tensor_tensor(z_rows[:, rows, :], lo[:, rows, :], mid[:, rows, :], ALU.max)
        z_bf, z_walk = packed_tile("z_bf", S)
        nc.vector.tensor_copy(z_walk, interleaved(z_rows[:]))
        z_c, z_s = quantize("z", z_bf, S)
        a_ps = [psum.tile([P, S], F32, name=f"a_ps{c}", tag=f"a{c}") for c in range(PACK)]
        for c in range(PACK):
            mx_product(a_ps[c][:], ca_w, ca_s, c, z_c[:], z_s[:])

        mx = [keep.tile([P, PACK, HALF], F32, name=f"mx{h}") for h in range(2)]
        th = [keep.tile([P, PACK, HALF], F32, name=f"th{h}") for h in range(2)]
        b_ps = [psum.tile([P, S], F32, name=f"b_ps{c}", tag=f"y_then_b{c}") for c in range(PACK)]

        def largest_and_tanh(t, h):
            mb = ring.tile([P, HALF, MEMBERS], F32, name="mb", bufs=MEMBER_BUFFERS)
            gather("scalar", mb[:].rearrange("p j m -> p (j m)"), y2[t][:], entries(n3_t, h * HALF * MEMBERS, HALF * MEMBERS))
            big = ring.tile([P, HALF, 2], F32, name="big")
            small = ring.tile([P, HALF, 2], F32, name="small")
            mn = ring.tile([P, HALF], F32, name="mn")
            diff = ring.tile([P, HALF], F32, name="diff", bufs=2 * PACK)
            nc.vector.tensor_tensor(small[:], mb[:, :, 0:2], mb[:, :, 2:4], ALU.min)
            nc.vector.tensor_tensor(big[:], mb[:, :, 0:2], mb[:, :, 2:4], ALU.max)
            nc.vector.tensor_tensor(mn[:], small[:, :, 0], small[:, :, 1], ALU.min)
            nc.vector.tensor_tensor(mx[h][:, t, :], big[:, :, 0], big[:, :, 1], ALU.max)
            nc.vector.tensor_tensor(diff[:], y2[t][:, h * HALF : (h + 1) * HALF], mn[:], ALU.subtract)
            nc.scalar.activation(th[h][:, t, :], diff[:], ACT.Tanh, scale=g2_inv[:, t : t + 1])

        def score_half(h):
            z2_bf, z2_walk = packed_tile(f"z2_{h}_bf", HALF)
            nc.vector.tensor_tensor(z2_walk, interleaved(mx[h][:]), interleaved(th[h][:]), ALU.mult)
            z2_c, z2_s = quantize(f"z2_{h}", z2_bf, HALF)
            for c in range(PACK):
                mx_product(b_ps[c][:, h * HALF : (h + 1) * HALF], cb_w, cb_s, c, z2_c[:], z2_s[:])

        for h in range(2):
            for t in range(PACK):
                largest_and_tanh(t, h)
                if (h, t) == (1, FIRST_HALF_SCORED_AFTER):
                    score_half(0)
        score_half(1)

        a_sb = [y2[0], y2[1], y2[3], y2[2]]
        a4 = []
        for c in range(PACK):
            engine = "scalar" if c < LAST else "vector"
            fetched = keep.tile([P, S], F32, name=f"a4_{c}", tag=f"a4_{c}" if c < LAST else "z2_1_bf", align_bytes=64)
            leave_bank(engine, a_sb[c][:, :S], a_ps[c][:], SIXTEENTH)
            gather(engine, fetched[:], a_sb[c][:], n4_t[:])
            a4.append(fetched)

        b_sb = y1
        b5 = keep.tile([P, PACK, S], F32, name="b5")
        less = keep.tile([P, PACK, S], F32, name="less")
        for c in range(PACK):
            leave_bank("scalar" if c < B_TILES_ON_SCALAR else "vector", b_sb[c][:], b_ps[c][:], SIXTEENTH)
        for c in range(PACK):
            for first in (0, HALF):
                gather("scalar", b5[:, c, first : first + HALF], b_sb[c][:], entries(n5_t, first, HALF))
            nc.vector.scalar_tensor_tensor(less[:, c, :], b_ps[c][:], SIXTEENTH, a4[c][:], ALU.mult, ALU.min)
            width = S if c < LAST else HALF
            subtractor = nc.gpsimd if c < LAST else nc.vector
            for first in range(0, S, width):
                cols = slice(first, first + width)
                more = ring.tile([P, width], F32, name="more", bufs=PACK + 1)
                res = ring.tile([P, width], F32, name="res", bufs=PACK + 1)
                nc.vector.scalar_tensor_tensor(more[:], a_ps[c][:, cols], SIXTEENTH, b5[:, c, cols], ALU.mult, ALU.max)
                subtractor.tensor_tensor(res[:], more[:], less[:, c, cols], ALU.subtract)
                nc.sync.dma_start(out[P * c : P * (c + 1), cols], res[:])
